import numpy as np
import ml_dtypes


def mxq(x, axis, fmt="e4m3"):
    dtype, down = {"e4m3": (ml_dtypes.float8_e4m3fn, 7), "e5m2": (ml_dtypes.float8_e5m2, 14)}[fmt]
    v = np.moveaxis(np.asarray(x, np.float32).astype(ml_dtypes.bfloat16).astype(np.float64), axis, -1)
    blocks = v.reshape(v.shape[:-1] + (-1, 32))
    amax = np.abs(blocks).max(-1, keepdims=True)
    byte = np.maximum(np.where(amax > 0, np.frexp(amax)[1] - 1 + 127, 0) - down, 1)
    scale = np.exp2(byte - 127.0)
    codes = (blocks / scale).astype(np.float32).astype(dtype).astype(np.float64)
    return np.moveaxis((codes * scale).reshape(v.shape), -1, axis)


WIDE = False


def mx_kscale(k):
    if not WIDE:
        return np.ones(k)
    levels = np.array([30, -30])
    if k % 512:
        return np.exp2(np.random.permutation(np.resize(levels, k // 32))).repeat(32)
    a = np.empty((k // 512, 16))
    for p in range(k // 512):
        a[p, :8] = np.random.permutation(np.resize(levels, 8))
        for g in range(8):
            far = levels[np.abs(levels - a[p, g]) >= 10]
            a[p, g + 8] = far[np.random.randint(len(far))]
    return np.exp2(a.ravel()).repeat(32)


def f64(x):
    return np.asarray(x).astype(np.float64)


def striped(idx):
    return np.tile(np.asarray(idx).reshape(-1, 16).T, (8, 1)).astype(np.uint16)


def unstriped(offs):
    return offs[:16].T.reshape(-1).astype(np.int64)


E2M1 = np.array([0.0, 0.5, 1.0, 1.5, 2.0, 3.0, 4.0, 6.0, -0.0, -0.5, -1.0, -1.5, -2.0, -3.0, -4.0, -6.0])


def pack_weight(w, fmt):
    k, n = w.shape
    w = f64(np.asarray(w, np.float32).astype(ml_dtypes.bfloat16)).reshape(k // 32, 32, n)
    amax = np.abs(w).max(1)
    if fmt in ("e4m3", "e5m2"):
        byte = np.frexp(amax)[1] - 1 + 127 - (7 if fmt == "e4m3" else 14)
    else:
        mant, ex = np.frexp(amax / 6.0)
        byte = np.where(mant > 0.5, ex, ex - 1) + 127
    byte = np.clip(np.where(amax > 0, byte, 1), 1, 254)
    scaled = (w * np.exp2(127.0 - byte)[:, None, :]).reshape(k, n).astype(np.float32)
    by_word = np.ascontiguousarray(scaled.reshape(k // 512, 128, 4, n).transpose(0, 1, 3, 2))
    if fmt in ("e4m3", "e5m2"):
        words = by_word.astype(ml_dtypes.float8_e4m3fn if fmt == "e4m3" else ml_dtypes.float8_e5m2).view(np.uint8)
    else:
        c = by_word.astype(ml_dtypes.float4_e2m1fn).view(np.uint8) & 0xF
        words = (c[..., 0::2] | (c[..., 1::2] << 4)).reshape(k // 512, 128, 2 * n)
    return np.ascontiguousarray(words), np.ascontiguousarray(byte.astype(np.uint8).reshape(k // 512, 16, n))


def unpack_weight(words, scales, fmt):
    g, _, n = scales.shape
    words = np.ascontiguousarray(words).reshape(g, 128, n, -1)
    if fmt in ("e4m3", "e5m2"):
        vals = words.view(ml_dtypes.float8_e4m3fn if fmt == "e4m3" else ml_dtypes.float8_e5m2).astype(np.float64)
    else:
        nib = np.empty((g, 128, n, 4), np.uint8)
        nib[..., 0::2] = words & 0xF
        nib[..., 1::2] = words >> 4
        vals = E2M1[nib]
    vals = vals * np.repeat(np.exp2(scales.astype(np.float64) - 127.0), 8, axis=1)[..., None]
    return vals.transpose(0, 1, 3, 2).reshape(g * 512, n)


K, F, T, Z, J, R, C, N, E = 512, 512, 1024, 1024, 256, 512, 512, 256, 1024


def setup_inputs():
    n = np.random.standard_normal
    idx = np.random.permutation(T)[:J]
    idx2 = np.random.permutation(Z)[:J]
    idx3 = np.random.permutation(C)[:J]
    idx4 = np.random.permutation(C)[:J]
    idx5 = np.random.permutation(E)[:J]
    fk = mx_kscale(K)
    fr = mx_kscale(R)
    ff = mx_kscale(F)
    xtp = pack_weight(n((K, T)) / fk[:, None], "e2m1")
    wp = pack_weight(n((K, R)) * 1 / np.sqrt(K) * fk[:, None] * fr, "e5m2")
    xop = pack_weight(n((F, Z)) / ff[:, None], "e5m2")
    w0p = pack_weight(n((F, R)) * 1 / np.sqrt(F) * ff[:, None] * fr, "e4m3")
    wbp = pack_weight(n((R, N)) * 1 / np.sqrt(R) / fr[:, None], "e4m3")
    return {
        "xt_words": xtp[0],
        "xt_scales": xtp[1],
        "w_words": wp[0],
        "w_scales": wp[1],
        "xo_words": xop[0],
        "xo_scales": xop[1],
        "w0_words": w0p[0],
        "w0_scales": w0p[1],
        "sa": (np.random.uniform(0.5, 1.6, (R, 1))).astype(np.float32),
        "wb_words": wbp[0],
        "wb_scales": wbp[1],
        "tz": (np.random.randint(-9, 10, (N, E)).astype(np.float64)).astype(np.float32),
        "so": (np.random.uniform(0.1, 0.3, (N, 1))).astype(np.float32),
        "offs": striped(idx),
        "offs2": striped(idx2),
        "offs3": striped(idx3),
        "offs4": striped(idx4),
        "offs5": striped(idx5),
    }


def reference(xt_words, xt_scales, w_words, w_scales, xo_words, xo_scales, w0_words, w0_scales, sa, wb_words, wb_scales, tz, so, offs, offs2, offs3, offs4, offs5):
    idx = unstriped(offs)
    idx2 = unstriped(offs2)
    idx3 = unstriped(offs3)
    idx4 = unstriped(offs4)
    idx5 = unstriped(offs5)
    xtu = unpack_weight(xt_words, xt_scales, "e2m1")
    wu = unpack_weight(w_words, w_scales, "e5m2")
    xou = unpack_weight(xo_words, xo_scales, "e5m2")
    w0u = unpack_weight(w0_words, w0_scales, "e4m3")
    wbu = unpack_weight(wb_words, wb_scales, "e4m3")
    xtidxg = xtu[:, idx]
    xoidx2g = xou[:, idx2]
    a = wu.T @ xtidxg + w0u.T @ xoidx2g
    pw = np.zeros((R, C))
    pw[:, idx3] = a
    hid = np.abs(pw[:, idx4] * f64(sa) - a)
    hidq = mxq(hid, 0, "e5m2")
    p = wbu.T @ hidq
    y = np.maximum(p, f64(tz)[:, idx5] * f64(so))
    return y

@@ -1,0 +1,198 @@
+from contextlib import ExitStack
+
+import concourse.mybir as mybir
+
+F32 = mybir.dt.float32
+BF16 = mybir.dt.bfloat16
+I32 = mybir.dt.int32
+U32 = mybir.dt.uint32
+U16 = mybir.dt.uint16
+U8 = mybir.dt.uint8
+E4M3 = mybir.dt.float8_e4m3fn_x4
+E5M2 = mybir.dt.float8_e5m2_x4
+E2M1 = mybir.dt.float4_e2m1fn_x4
+ALU = mybir.AluOpType
+ACT = mybir.ActivationFunctionType
+
+K, F, T, Z, J, R, C, N, E = 512, 512, 1024, 1024, 256, 512, 512, 256, 1024
+P = 128
+PACK = 4
+QUADS = 4
+QUAD = 32
+FLOPS = 2 * K * R * J + 2 * F * R * J + 2 * R * N * J
+
+
+def words_of(packed):
+    return packed[0].rearrange("p n t -> p (n t)").bitcast(I32)
+
+
+def tile_list_boardownweighed_bank_one_stepfloor_kernel(
+    tc, xt_words, xt_scales, w_words, w_scales, xo_words, xo_scales, w0_words, w0_scales, sa,
+    wb_words, wb_scales, tz, so, offs, offs2, offs3, offs4, offs5, out,
+):
+    nc = tc.nc
+    with ExitStack() as ctx:
+        sb = ctx.enter_context(tc.tile_pool(name="sb", bufs=1))
+        ps = ctx.enter_context(tc.psum_pool(name="ps", bufs=1))
+
+        def new(name, shape, dtype):
+            return sb.tile(shape, dtype, name=name, align_bytes=64)
+
+        def load_list(name, src):
+            t = new(name, [P, J // 16], U16)
+            nc.sync.dma_start(t[:], src)
+            return t
+
+        def load_plane(queue, plane, scales):
+            rows = scales[0].bitcast(I32)
+            for q in range(QUADS):
+                queue.dma_start(plane[QUAD * q : QUAD * q + PACK, :].bitcast(I32), rows[PACK * q : PACK * (q + 1), :])
+
+        def rows_by_quadrant(scales):
+            return scales[0].bitcast(I32).rearrange("(q r) n -> r q n", r=PACK)
+
+        def spread(plane, stage):
+            for q in range(QUADS):
+                nc.vector.tensor_copy(plane[QUAD * q : QUAD * q + PACK, :].bitcast(I32), stage[:, q, :])
+
+        xt_plane = new("xt_plane", [P, T], U8)
+        xo_plane = new("xo_plane", [P, Z], U8)
+        ww_plane = new("ww_plane", [P, 2 * R], U8)
+        wb_plane = new("wb_plane", [P, N], U8)
+        board = [new("board%d" % t, [P, C], F32) for t in range(PACK)]
+        nc.gpsimd.memset(xo_plane[:].bitcast(I32), 0)
+        nc.vector.memset(xt_plane[:].bitcast(I32), 0)
+        nc.vector.memset(ww_plane[:].bitcast(I32), 0)
+        for t in range(PACK):
+            (nc.vector, nc.gpsimd)[t // 2].memset(board[t][:], 0.0)
+        nc.gpsimd.memset(wb_plane[:].bitcast(I32), 0)
+
+        xt_stage = new("xt_stage", [PACK, QUADS, T // 4], I32)
+        ww_stage = new("ww_stage", [PACK, QUADS, 2 * R // 4], I32)
+        xt_tab = new("xt_tab", [P, T], U16)
+        xo_tab = new("xo_tab", [P, Z], U32)
+        w_raw = new("w_raw", [P, R], U32)
+        w0_raw = new("w0_raw", [P, R], U32)
+        tz_rows = [new("tz%d" % h, [P, E], F32) for h in range(2)]
+        wb_codes = new("wb_codes", [P, N], U32)
+        so_cols = new("so_cols", [P, 2], F32)
+        sa_cols = new("sa_cols", [P, PACK], F32)
+
+        l1 = load_list("l1", offs)
+        nc.scalar.dma_start(xt_tab[:].bitcast(I32), xt_words[0].bitcast(I32))
+        nc.sync.dma_start(xt_stage[:], rows_by_quadrant(xt_scales))
+        nc.scalar.dma_start(xo_tab[:].bitcast(I32), words_of(xo_words))
+        nc.sync.dma_start(ww_stage[:, :, 0 : R // 4], rows_by_quadrant(w_scales))
+        nc.scalar.dma_start(w_raw[:].bitcast(I32), words_of(w_words))
+        nc.sync.dma_start(ww_stage[:, :, R // 4 : R // 2], rows_by_quadrant(w0_scales))
+        nc.scalar.dma_start(w0_raw[:].bitcast(I32), words_of(w0_words))
+        l2 = load_list("l2", offs2)
+        nc.sync.dma_start(tz_rows[0][:], tz[0:P, :])
+        load_plane(nc.sync, xo_plane, xo_scales)
+        l5 = load_list("l5", offs5)
+        with nc.allow_non_contiguous_dma(reason="one value a partition and half"):
+            nc.sync.dma_start(so_cols[:], so.rearrange("(h p) o -> p (h o)", p=P))
+        l3 = load_list("l3", offs3)
+        l4 = load_list("l4", offs4)
+        nc.sync.dma_start(sa_cols[:], sa.rearrange("(p t) o -> p (t o)", t=PACK))
+        nc.sync.dma_start(tz_rows[1][:], tz[P : 2 * P, :])
+        nc.sync.dma_start(wb_codes[:].bitcast(I32), words_of(wb_words))
+        load_plane(nc.sync, wb_plane, wb_scales)
+
+        xt_codes = new("xt_codes", [P, J], U16)
+        xt_sc = new("xt_sc", [P, J], U8)
+        xo_codes = new("xo_codes", [P, J], U32)
+        xo_sc = new("xo_sc", [P, J], U8)
+        ww_sc = [new("ww_sc%d" % u, [P, 2, 2 * P], U8) for u in range(2)]
+
+        def deal_scales(u):
+            nc.vector.tensor_copy(
+                ww_sc[u][:].rearrange("p i (t m) -> p i m t", t=2),
+                ww_plane[:].rearrange("p (i m t) -> p i m t", i=2, t=PACK)[:, :, :, 2 * u : 2 * u + 2],
+            )
+
+        nc.vector.tensor_copy(xt_codes[:], xt_tab[:].indirect(l1[:]))
+        spread(xt_plane, xt_stage)
+        spread(ww_plane, ww_stage)
+        nc.vector.tensor_copy(xt_sc[:], xt_plane[:].indirect(l1[:]))
+        deal_scales(0)
+        nc.vector.tensor_copy(xo_codes[:], xo_tab[:].indirect(l2[:]))
+        nc.vector.tensor_copy(xo_sc[:], xo_plane[:].indirect(l2[:]))
+        deal_scales(1)
+
+        w_codes = new("w_codes", [P, R], U32)
+        w0_codes = new("w0_codes", [P, R], U32)
+        for codes, raw in ((w_codes, w_raw), (w0_codes, w0_raw)):
+            nc.scalar.copy(codes[:].rearrange("p (t m) -> p m t", t=PACK), raw[:].rearrange("p (m t) -> p m t", t=PACK))
+
+        a_ps = [ps.tile([P, J], F32, name="a_ps%d" % t) for t in range(PACK)]
+        for u in range(2):
+            for i, (codes, fmt, moving, moving_sc) in enumerate((
+                (w_codes, E5M2, xt_codes[:].bitcast(E2M1), xt_sc), (w0_codes, E4M3, xo_codes[:].bitcast(E5M2), xo_sc),
+            )):
+                for v in range(2):
+                    t = 2 * u + v
+                    nc.tensor.matmul_mx(
+                        a_ps[t][:], lhsT=codes[:, P * t : P * (t + 1)].bitcast(fmt),
+                        lhsT_scale=ww_sc[u][:, i, P * v : P * (v + 1)],
+                        rhs=moving, rhs_scale=moving_sc[:], start=(i == 0), stop=(i == 1),
+                    )
+
+        a01 = new("a01", [P, 2, J], F32)
+        got = new("got", [P, PACK, J], F32)
+        diff = new("diff", [P, PACK, J], F32)
+        floor = new("floor", [P, 2, J], F32)
+        a = [a01[:, 0, :], a01[:, 1, :], floor[:, 1, :], diff[:, 0, :]]
+        H = J // 2
+
+        def fetch(t, first, count):
+            nc.scalar.activation(
+                got[:, t, first : first + count], board[t][:].indirect(l4[:, first // 16 : (first + count) // 16]),
+                ACT.Copy, scale=sa_cols[:, t : t + 1],
+            )
+
+        def fetch_floor(h):
+            nc.scalar.activation(floor[:, h, :], tz_rows[h][:].indirect(l5[:]), ACT.Copy, scale=so_cols[:, h : h + 1])
+
+        fetch_floor(0)
+        nc.scalar.copy(a[0], a_ps[0][:])
+        nc.vector.tensor_copy(a[1], a_ps[1][:])
+        nc.scalar.activation(board[0][:].indirect(l3[:]), a[0], ACT.Copy)
+        nc.vector.tensor_copy(a[2], a_ps[2][:])
+        nc.vector.tensor_copy(board[1][:].indirect(l3[:]), a[1])
+        nc.vector.tensor_copy(a[3], a_ps[3][:])
+        nc.scalar.activation(board[2][:].indirect(l3[:]), a[2], ACT.Copy)
+        nc.vector.tensor_copy(board[3][:].indirect(l3[:]), a[3])
+        fetch(0, 0, J)
+        fetch(1, 0, J)
+        nc.vector.tensor_tensor(diff[:, 0:2, :], got[:, 0:2, :], a01[:], ALU.subtract)
+        for s in range(2):
+            js = slice(H * s, H * (s + 1))
+            for t in (2, 3):
+                fetch(t, H * s, H)
+                nc.vector.tensor_tensor(diff[:, t, js], got[:, t, js], a_ps[t][:, js], ALU.subtract)
+        hid = [new("hid%d" % s, [P, H * PACK], BF16) for s in range(2)]
+        for s in range(2):
+            nc.scalar.activation(
+                hid[s][:].rearrange("p (c i t) -> p c t i", i=4, t=PACK),
+                diff[:, :, H * s : H * (s + 1)].rearrange("p t (c i) -> p c t i", i=4),
+                ACT.Abs,
+            )
+        fetch_floor(1)
+
+        out_rows = out.rearrange("(h p) j -> p h j", p=P)
+        for s in range(2):
+            js = slice(H * s, H * (s + 1))
+            hid_codes = new("hid_codes%d" % s, [P, H], U32)
+            hid_sc = new("hid_sc%d" % s, [P, H], U8)
+            nc.vector.quantize_mx(hid_codes[:].bitcast(E5M2), hid_sc[:], hid[s][:])
+            p_ps = ps.tile([P, 2, H], F32, name="p_ps%d" % s)
+            for h in range(2):
+                cols = slice(P * h, P * (h + 1))
+                nc.tensor.matmul_mx(
+                    p_ps[:, h, :], lhsT=wb_codes[:, cols].bitcast(E4M3), lhsT_scale=wb_plane[:, cols],
+                    rhs=hid_codes[:].bitcast(E5M2), rhs_scale=hid_sc[:], start=True, stop=True,
+                )
+            y = new("y%d" % s, [P, 2, H], F32)
+            nc.vector.tensor_tensor(y[:], p_ps[:], floor[:, :, js], ALU.max)
+            nc.sync.dma_start(out_rows[:, :, js], y[:])

@@ -80,18 +80,18 @@ def tile_list_boardownweighed_bank_one_stepfloor_kernel(
 
         l1 = load_list("l1", offs)
         nc.scalar.dma_start(xt_tab[:].bitcast(I32), xt_words[0].bitcast(I32))
-        nc.sync.dma_start(xt_stage[:], rows_by_quadrant(xt_scales))
-        nc.scalar.dma_start(xo_tab[:].bitcast(I32), words_of(xo_words))
         nc.sync.dma_start(ww_stage[:, :, 0 : R // 4], rows_by_quadrant(w_scales))
         nc.scalar.dma_start(w_raw[:].bitcast(I32), words_of(w_words))
         nc.sync.dma_start(ww_stage[:, :, R // 4 : R // 2], rows_by_quadrant(w0_scales))
+        nc.scalar.dma_start(xo_tab[:].bitcast(I32), words_of(xo_words))
+        nc.sync.dma_start(xt_stage[:], rows_by_quadrant(xt_scales))
         nc.scalar.dma_start(w0_raw[:].bitcast(I32), words_of(w0_words))
         l2 = load_list("l2", offs2)
-        nc.sync.dma_start(tz_rows[0][:], tz[0:P, :])
         load_plane(nc.sync, xo_plane, xo_scales)
-        l5 = load_list("l5", offs5)
+        nc.sync.dma_start(tz_rows[0][:], tz[0:P, :])
         with nc.allow_non_contiguous_dma(reason="one value a partition and half"):
             nc.sync.dma_start(so_cols[:], so.rearrange("(h p) o -> p (h o)", p=P))
+        l5 = load_list("l5", offs5)
         l3 = load_list("l3", offs3)
         l4 = load_list("l4", offs4)
         nc.sync.dma_start(sa_cols[:], sa.rearrange("(p t) o -> p (t o)", t=PACK))
@@ -103,7 +103,7 @@ def tile_list_boardownweighed_bank_one_stepfloor_kernel(
         xt_sc = new("xt_sc", [P, J], U8)
         xo_codes = new("xo_codes", [P, J], U32)
         xo_sc = new("xo_sc", [P, J], U8)
-        ww_sc = [new("ww_sc%d" % u, [P, 2, 2 * P], U8) for u in range(2)]
+        ww_sc = [new("ww_sc0", [P, 2, 2 * P], U8), sb.tile([P, 2, 2 * P], U8, name="ww_sc1", tag="xo_plane", align_bytes=64)]
 
         def deal_scales(u):
             nc.vector.tensor_copy(
@@ -112,10 +112,10 @@ def tile_list_boardownweighed_bank_one_stepfloor_kernel(
             )
 
         nc.vector.tensor_copy(xt_codes[:], xt_tab[:].indirect(l1[:]))
-        spread(xt_plane, xt_stage)
         spread(ww_plane, ww_stage)
-        nc.vector.tensor_copy(xt_sc[:], xt_plane[:].indirect(l1[:]))
+        spread(xt_plane, xt_stage)
         deal_scales(0)
+        nc.vector.tensor_copy(xt_sc[:], xt_plane[:].indirect(l1[:]))
         nc.vector.tensor_copy(xo_codes[:], xo_tab[:].indirect(l2[:]))
         nc.vector.tensor_copy(xo_sc[:], xo_plane[:].indirect(l2[:]))
         deal_scales(1)
@@ -126,23 +126,25 @@ def tile_list_boardownweighed_bank_one_stepfloor_kernel(
             nc.scalar.copy(codes[:].rearrange("p (t m) -> p m t", t=PACK), raw[:].rearrange("p (m t) -> p m t", t=PACK))
 
         a_ps = [ps.tile([P, J], F32, name="a_ps%d" % t) for t in range(PACK)]
-        for u in range(2):
-            for i, (codes, fmt, moving, moving_sc) in enumerate((
-                (w_codes, E5M2, xt_codes[:].bitcast(E2M1), xt_sc), (w0_codes, E4M3, xo_codes[:].bitcast(E5M2), xo_sc),
-            )):
-                for v in range(2):
-                    t = 2 * u + v
-                    nc.tensor.matmul_mx(
-                        a_ps[t][:], lhsT=codes[:, P * t : P * (t + 1)].bitcast(fmt),
-                        lhsT_scale=ww_sc[u][:, i, P * v : P * (v + 1)],
-                        rhs=moving, rhs_scale=moving_sc[:], start=(i == 0), stop=(i == 1),
-                    )
+        products = ((w_codes, E5M2, xt_codes[:].bitcast(E2M1), xt_sc), (w0_codes, E4M3, xo_codes[:].bitcast(E5M2), xo_sc))
+        for t, i in ((0, 0), (1, 0), (0, 1), (2, 0), (2, 1), (1, 1), (3, 0), (3, 1)):
+            codes, fmt, moving, moving_sc = products[i]
+            nc.tensor.matmul_mx(
+                a_ps[t][:], lhsT=codes[:, P * t : P * (t + 1)].bitcast(fmt),
+                lhsT_scale=ww_sc[t // 2][:, i, P * (t % 2) : P * (t % 2 + 1)],
+                rhs=moving, rhs_scale=moving_sc[:], start=(i == 0), stop=(i == 1),
+            )
 
+        def fetch_floor(floor, h):
+            nc.scalar.activation(floor[:], tz_rows[h][:].indirect(l5[:]), ACT.Copy, scale=so_cols[:, h : h + 1])
+
+        floor0 = new("floor0", [P, J], F32)
+        fetch_floor(floor0, 0)
         a01 = new("a01", [P, 2, J], F32)
+        a2 = new("a2", [P, J], F32)
         got = new("got", [P, PACK, J], F32)
         diff = new("diff", [P, PACK, J], F32)
-        floor = new("floor", [P, 2, J], F32)
-        a = [a01[:, 0, :], a01[:, 1, :], floor[:, 1, :], diff[:, 0, :]]
+        a = [a01[:, 0, :], a01[:, 1, :], a2[:], diff[:].rearrange("p t j -> p (t j)")[:, J // 2 : J // 2 + J]]
         H = J // 2
 
         def fetch(t, first, count):
@@ -151,21 +153,15 @@ def tile_list_boardownweighed_bank_one_stepfloor_kernel(
                 ACT.Copy, scale=sa_cols[:, t : t + 1],
             )
 
-        def fetch_floor(h):
-            nc.scalar.activation(floor[:, h, :], tz_rows[h][:].indirect(l5[:]), ACT.Copy, scale=so_cols[:, h : h + 1])
-
-        fetch_floor(0)
-        nc.scalar.copy(a[0], a_ps[0][:])
-        nc.vector.tensor_copy(a[1], a_ps[1][:])
-        nc.scalar.activation(board[0][:].indirect(l3[:]), a[0], ACT.Copy)
-        nc.vector.tensor_copy(a[2], a_ps[2][:])
-        nc.vector.tensor_copy(board[1][:].indirect(l3[:]), a[1])
-        nc.vector.tensor_copy(a[3], a_ps[3][:])
-        nc.scalar.activation(board[2][:].indirect(l3[:]), a[2], ACT.Copy)
-        nc.vector.tensor_copy(board[3][:].indirect(l3[:]), a[3])
-        fetch(0, 0, J)
-        fetch(1, 0, J)
-        nc.vector.tensor_tensor(diff[:, 0:2, :], got[:, 0:2, :], a01[:], ALU.subtract)
+        for t in (0, 2, 1, 3):
+            nc.vector.tensor_copy(a[t], a_ps[t][:])
+        for t in range(2):
+            nc.scalar.activation(board[t][:].indirect(l3[:]), a[t], ACT.Copy)
+        for t in range(2, PACK):
+            nc.vector.tensor_copy(board[t][:].indirect(l3[:]), a[t])
+        for t in range(2):
+            fetch(t, 0, J)
+            nc.vector.tensor_tensor(diff[:, t, :], got[:, t, :], a[t], ALU.subtract)
         for s in range(2):
             js = slice(H * s, H * (s + 1))
             for t in (2, 3):
@@ -178,21 +174,22 @@ def tile_list_boardownweighed_bank_one_stepfloor_kernel(
                 diff[:, :, H * s : H * (s + 1)].rearrange("p t (c i) -> p c t i", i=4),
                 ACT.Abs,
             )
-        fetch_floor(1)
+        floor1 = sb.tile([P, J], F32, name="floor1", tag="a01", align_bytes=64)
+        fetch_floor(floor1, 1)
 
-        out_rows = out.rearrange("(h p) j -> p h j", p=P)
+        out_rows = out
+        p_ps = [ps.tile([P, J], F32, name="p_ps%d" % h) for h in range(2)]
         for s in range(2):
-            js = slice(H * s, H * (s + 1))
             hid_codes = new("hid_codes%d" % s, [P, H], U32)
             hid_sc = new("hid_sc%d" % s, [P, H], U8)
             nc.vector.quantize_mx(hid_codes[:].bitcast(E5M2), hid_sc[:], hid[s][:])
-            p_ps = ps.tile([P, 2, H], F32, name="p_ps%d" % s)
             for h in range(2):
                 cols = slice(P * h, P * (h + 1))
                 nc.tensor.matmul_mx(
-                    p_ps[:, h, :], lhsT=wb_codes[:, cols].bitcast(E4M3), lhsT_scale=wb_plane[:, cols],
+                    p_ps[h][:, H * s : H * (s + 1)], lhsT=wb_codes[:, cols].bitcast(E4M3), lhsT_scale=wb_plane[:, cols],
                     rhs=hid_codes[:].bitcast(E5M2), rhs_scale=hid_sc[:], start=True, stop=True,
                 )
-            y = new("y%d" % s, [P, 2, H], F32)
-            nc.vector.tensor_tensor(y[:], p_ps[:], floor[:, :, js], ALU.max)
-            nc.sync.dma_start(out_rows[:, :, js], y[:])
+        for h in range(2):
+            y = new("y%d" % h, [P, J], F32)
+            nc.vector.tensor_tensor(y[:], p_ps[h][:], (floor0, floor1)[h][:], ALU.max)
+            nc.sync.dma_start(out[P * h : P * (h + 1), :], y[:])

@@ -88,14 +88,14 @@ def tile_list_boardownweighed_bank_one_stepfloor_kernel(
         nc.scalar.dma_start(w0_raw[:].bitcast(I32), words_of(w0_words))
         l2 = load_list("l2", offs2)
         load_plane(nc.sync, xo_plane, xo_scales)
-        nc.sync.dma_start(tz_rows[0][:], tz[0:P, :])
-        with nc.allow_non_contiguous_dma(reason="one value a partition and half"):
-            nc.sync.dma_start(so_cols[:], so.rearrange("(h p) o -> p (h o)", p=P))
-        l5 = load_list("l5", offs5)
         l3 = load_list("l3", offs3)
         l4 = load_list("l4", offs4)
         nc.sync.dma_start(sa_cols[:], sa.rearrange("(p t) o -> p (t o)", t=PACK))
-        nc.sync.dma_start(tz_rows[1][:], tz[P : 2 * P, :])
+        for h in range(2):
+            nc.sync.dma_start(tz_rows[h][:], tz[P * h : P * (h + 1), :])
+        l5 = load_list("l5", offs5)
+        with nc.allow_non_contiguous_dma(reason="one value a partition and half"):
+            nc.sync.dma_start(so_cols[:], so.rearrange("(h p) o -> p (h o)", p=P))
         nc.sync.dma_start(wb_codes[:].bitcast(I32), words_of(wb_words))
         load_plane(nc.sync, wb_plane, wb_scales)
 
@@ -135,11 +135,6 @@ def tile_list_boardownweighed_bank_one_stepfloor_kernel(
                 rhs=moving, rhs_scale=moving_sc[:], start=(i == 0), stop=(i == 1),
             )
 
-        def fetch_floor(floor, h):
-            nc.scalar.activation(floor[:], tz_rows[h][:].indirect(l5[:]), ACT.Copy, scale=so_cols[:, h : h + 1])
-
-        floor0 = new("floor0", [P, J], F32)
-        fetch_floor(floor0, 0)
         a01 = new("a01", [P, 2, J], F32)
         a2 = new("a2", [P, J], F32)
         got = new("got", [P, PACK, J], F32)
@@ -153,7 +148,8 @@ def tile_list_boardownweighed_bank_one_stepfloor_kernel(
                 ACT.Copy, scale=sa_cols[:, t : t + 1],
             )
 
-        for t in (0, 2, 1, 3):
+        nc.scalar.copy(a[0], a_ps[0][:])
+        for t in (2, 1, 3):
             nc.vector.tensor_copy(a[t], a_ps[t][:])
         for t in range(2):
             nc.scalar.activation(board[t][:].indirect(l3[:]), a[t], ACT.Copy)
@@ -174,8 +170,9 @@ def tile_list_boardownweighed_bank_one_stepfloor_kernel(
                 diff[:, :, H * s : H * (s + 1)].rearrange("p t (c i) -> p c t i", i=4),
                 ACT.Abs,
             )
-        floor1 = sb.tile([P, J], F32, name="floor1", tag="a01", align_bytes=64)
-        fetch_floor(floor1, 1)
+        floor = sb.tile([P, 2, J], F32, name="floor", tag="a01", align_bytes=64)
+        for h in range(2):
+            nc.scalar.activation(floor[:, h, :], tz_rows[h][:].indirect(l5[:]), ACT.Copy, scale=so_cols[:, h : h + 1])
 
         out_rows = out
         p_ps = [ps.tile([P, J], F32, name="p_ps%d" % h) for h in range(2)]
@@ -191,5 +188,5 @@ def tile_list_boardownweighed_bank_one_stepfloor_kernel(
                 )
         for h in range(2):
             y = new("y%d" % h, [P, J], F32)
-            nc.vector.tensor_tensor(y[:], p_ps[h][:], (floor0, floor1)[h][:], ALU.max)
+            nc.vector.tensor_tensor(y[:], p_ps[h][:], floor[:, h, :], ALU.max)
             nc.sync.dma_start(out[P * h : P * (h + 1), :], y[:])

@@ -19,6 +19,10 @@ P = 128
 PACK = 4
 QUADS = 4
 QUAD = 32
+PER_COLUMN = 16
+LINE = 4
+HALF = J // 2
+ALIGN = 64
 FLOPS = 2 * K * R * J + 2 * F * R * J + 2 * R * N * J
 
 
@@ -26,30 +30,37 @@ def words_of(packed):
     return packed[0].rearrange("p n t -> p (n t)").bitcast(I32)
 
 
+def rows_by_quadrant(scales):
+    return scales[0].bitcast(I32).rearrange("(q i) n -> i q n", i=PACK)
+
+
 def tile_list_boardownweighed_bank_one_stepfloor_kernel(
     tc, xt_words, xt_scales, w_words, w_scales, xo_words, xo_scales, w0_words, w0_scales, sa,
     wb_words, wb_scales, tz, so, offs, offs2, offs3, offs4, offs5, out,
 ):
     nc = tc.nc
+    halves = [slice(HALF * s, HALF * (s + 1)) for s in range(2)]
+    whole = slice(0, J)
+
     with ExitStack() as ctx:
         sb = ctx.enter_context(tc.tile_pool(name="sb", bufs=1))
         ps = ctx.enter_context(tc.psum_pool(name="ps", bufs=1))
 
         def new(name, shape, dtype):
-            return sb.tile(shape, dtype, name=name, align_bytes=64)
+            return sb.tile(shape, dtype, name=name, align_bytes=ALIGN)
 
         def load_list(name, src):
-            t = new(name, [P, J // 16], U16)
-            nc.sync.dma_start(t[:], src)
-            return t
+            entries = new(name, [P, J // PER_COLUMN], U16)
+            nc.sync.dma_start(entries[:], src)
+            return entries
 
-        def load_plane(queue, plane, scales):
+        def offsets(entries, slots):
+            return entries[:, slots.start // PER_COLUMN : slots.stop // PER_COLUMN]
+
+        def load_plane(plane, scales):
             rows = scales[0].bitcast(I32)
             for q in range(QUADS):
-                queue.dma_start(plane[QUAD * q : QUAD * q + PACK, :].bitcast(I32), rows[PACK * q : PACK * (q + 1), :])
-
-        def rows_by_quadrant(scales):
-            return scales[0].bitcast(I32).rearrange("(q r) n -> r q n", r=PACK)
+                nc.sync.dma_start(plane[QUAD * q : QUAD * q + PACK, :].bitcast(I32), rows[PACK * q : PACK * (q + 1), :])
 
         def spread(plane, stage):
             for q in range(QUADS):
@@ -78,112 +89,121 @@ def tile_list_boardownweighed_bank_one_stepfloor_kernel(
         so_cols = new("so_cols", [P, 2], F32)
         sa_cols = new("sa_cols", [P, PACK], F32)
 
-        l1 = load_list("l1", offs)
-        nc.scalar.dma_start(xt_tab[:].bitcast(I32), xt_words[0].bitcast(I32))
+        by_token = load_list("by_token", offs)
         nc.sync.dma_start(ww_stage[:, :, 0 : R // 4], rows_by_quadrant(w_scales))
-        nc.scalar.dma_start(w_raw[:].bitcast(I32), words_of(w_words))
         nc.sync.dma_start(ww_stage[:, :, R // 4 : R // 2], rows_by_quadrant(w0_scales))
-        nc.scalar.dma_start(xo_tab[:].bitcast(I32), words_of(xo_words))
         nc.sync.dma_start(xt_stage[:], rows_by_quadrant(xt_scales))
-        nc.scalar.dma_start(w0_raw[:].bitcast(I32), words_of(w0_words))
-        l2 = load_list("l2", offs2)
-        load_plane(nc.sync, xo_plane, xo_scales)
-        l3 = load_list("l3", offs3)
-        l4 = load_list("l4", offs4)
+        nc.sync.dma_start(xt_tab[:].bitcast(I32), xt_words[0].bitcast(I32))
+        nc.sync.dma_start(w_raw[:].bitcast(I32), words_of(w_words))
+        nc.sync.dma_start(xo_tab[:].bitcast(I32), words_of(xo_words))
+        nc.sync.dma_start(w0_raw[:].bitcast(I32), words_of(w0_words))
+        by_note = load_list("by_note", offs2)
+        load_plane(xo_plane, xo_scales)
+        to_board = load_list("to_board", offs3)
+        from_board = load_list("from_board", offs4)
         nc.sync.dma_start(sa_cols[:], sa.rearrange("(p t) o -> p (t o)", t=PACK))
         for h in range(2):
             nc.sync.dma_start(tz_rows[h][:], tz[P * h : P * (h + 1), :])
-        l5 = load_list("l5", offs5)
-        with nc.allow_non_contiguous_dma(reason="one value a partition and half"):
+        by_entry = load_list("by_entry", offs5)
+        with nc.allow_non_contiguous_dma(reason="one value for each partition and half of the output rows"):
             nc.sync.dma_start(so_cols[:], so.rearrange("(h p) o -> p (h o)", p=P))
         nc.sync.dma_start(wb_codes[:].bitcast(I32), words_of(wb_words))
-        load_plane(nc.sync, wb_plane, wb_scales)
+        load_plane(wb_plane, wb_scales)
 
         xt_codes = new("xt_codes", [P, J], U16)
         xt_sc = new("xt_sc", [P, J], U8)
         xo_codes = new("xo_codes", [P, J], U32)
         xo_sc = new("xo_sc", [P, J], U8)
-        ww_sc = [new("ww_sc0", [P, 2, 2 * P], U8), sb.tile([P, 2, 2 * P], U8, name="ww_sc1", tag="xo_plane", align_bytes=64)]
-
-        def deal_scales(u):
-            nc.vector.tensor_copy(
-                ww_sc[u][:].rearrange("p i (t m) -> p i m t", t=2),
-                ww_plane[:].rearrange("p (i m t) -> p i m t", i=2, t=PACK)[:, :, :, 2 * u : 2 * u + 2],
-            )
-
-        nc.vector.tensor_copy(xt_codes[:], xt_tab[:].indirect(l1[:]))
+        ww_sc = new("ww_sc", [P, 2, R], U8)
         spread(ww_plane, ww_stage)
         spread(xt_plane, xt_stage)
-        deal_scales(0)
-        nc.vector.tensor_copy(xt_sc[:], xt_plane[:].indirect(l1[:]))
-        nc.vector.tensor_copy(xo_codes[:], xo_tab[:].indirect(l2[:]))
-        nc.vector.tensor_copy(xo_sc[:], xo_plane[:].indirect(l2[:]))
-        deal_scales(1)
+        nc.vector.tensor_copy(
+            ww_sc[:].rearrange("p i (t m) -> p i t m", t=PACK),
+            ww_plane[:].rearrange("p (i m t) -> p i t m", i=2, t=PACK),
+        )
+        nc.vector.tensor_copy(xt_sc[:], xt_plane[:].indirect(by_token[:]))
+        nc.vector.tensor_copy(xt_codes[:], xt_tab[:].indirect(by_token[:]))
+        for slots in halves:
+            nc.vector.tensor_copy(xo_codes[:, slots], xo_tab[:].indirect(offsets(by_note, slots)))
+            nc.vector.tensor_copy(xo_sc[:, slots], xo_plane[:].indirect(offsets(by_note, slots)))
 
         w_codes = new("w_codes", [P, R], U32)
         w0_codes = new("w0_codes", [P, R], U32)
-        for codes, raw in ((w_codes, w_raw), (w0_codes, w0_raw)):
-            nc.scalar.copy(codes[:].rearrange("p (t m) -> p m t", t=PACK), raw[:].rearrange("p (m t) -> p m t", t=PACK))
+        nc.scalar.copy(w_codes[:].rearrange("p (t m) -> p m t", t=PACK), w_raw[:].rearrange("p (m t) -> p m t", t=PACK))
+        for u in range(2):
+            nc.scalar.copy(
+                w0_codes[:, 2 * P * u : 2 * P * (u + 1)].rearrange("p (t m) -> p m t", t=2),
+                w0_raw[:].rearrange("p (m t) -> p m t", t=PACK)[:, :, 2 * u : 2 * u + 2],
+            )
 
-        a_ps = [ps.tile([P, J], F32, name="a_ps%d" % t) for t in range(PACK)]
-        products = ((w_codes, E5M2, xt_codes[:].bitcast(E2M1), xt_sc), (w0_codes, E4M3, xo_codes[:].bitcast(E5M2), xo_sc))
-        for t, i in ((0, 0), (1, 0), (0, 1), (2, 0), (2, 1), (1, 1), (3, 0), (3, 1)):
-            codes, fmt, moving, moving_sc = products[i]
+        products = ((w_codes, E5M2, xt_codes, E2M1, xt_sc), (w0_codes, E4M3, xo_codes, E5M2, xo_sc))
+
+        def multiply(acc, t, i, slots):
+            codes, fmt, picked, picked_fmt, picked_sc = products[i]
             nc.tensor.matmul_mx(
-                a_ps[t][:], lhsT=codes[:, P * t : P * (t + 1)].bitcast(fmt),
-                lhsT_scale=ww_sc[t // 2][:, i, P * (t % 2) : P * (t % 2 + 1)],
-                rhs=moving, rhs_scale=moving_sc[:], start=(i == 0), stop=(i == 1),
+                acc[:], lhsT=codes[:, P * t : P * (t + 1)].bitcast(fmt), lhsT_scale=ww_sc[:, i, P * t : P * (t + 1)],
+                rhs=picked[:, slots].bitcast(picked_fmt), rhs_scale=picked_sc[:, slots], start=(i == 0), stop=(i == 1),
             )
 
         a01 = new("a01", [P, 2, J], F32)
-        a2 = new("a2", [P, J], F32)
+        a = [a01[:, 0, :], a01[:, 1, :]] + [new("a%d" % t, [P, J], F32)[:] for t in (2, 3)]
+        a0_ps = [ps.tile([P, HALF], F32, name="a0_ps%d" % s) for s in range(2)]
+        a_ps = {t: ps.tile([P, J], F32, name="a_ps%d" % t) for t in (1, 2)}
+        for i in range(2):
+            for s in range(2):
+                multiply(a0_ps[s], 0, i, halves[s])
+            for t in (1, 2):
+                multiply(a_ps[t], t, i, whole)
+        nc.scalar.copy(a01[:, 0, halves[0]], a0_ps[0][:])
+        a_ps[3] = ps.tile([P, J], F32, name="a_ps3", tag="a0_ps0")
+        for i in range(2):
+            multiply(a_ps[3], 3, i, whole)
+        nc.vector.tensor_copy(a01[:, 0, halves[1]], a0_ps[1][:])
+        for t in range(1, PACK):
+            nc.vector.tensor_copy(a[t], a_ps[t][:])
+
+        for slots in halves:
+            nc.scalar.activation(board[0][:].indirect(offsets(to_board, slots)), a01[:, 0, slots], ACT.Copy)
+        nc.scalar.activation(board[2][:].indirect(to_board[:]), a[2], ACT.Copy)
+        for t in (1, 3):
+            nc.vector.tensor_copy(board[t][:].indirect(to_board[:]), a[t])
+
         got = new("got", [P, PACK, J], F32)
         diff = new("diff", [P, PACK, J], F32)
-        a = [a01[:, 0, :], a01[:, 1, :], a2[:], diff[:].rearrange("p t j -> p (t j)")[:, J // 2 : J // 2 + J]]
-        H = J // 2
 
-        def fetch(t, first, count):
+        def fetch(t, slots):
             nc.scalar.activation(
-                got[:, t, first : first + count], board[t][:].indirect(l4[:, first // 16 : (first + count) // 16]),
-                ACT.Copy, scale=sa_cols[:, t : t + 1],
+                got[:, t, slots], board[t][:].indirect(offsets(from_board, slots)), ACT.Copy, scale=sa_cols[:, t : t + 1]
             )
 
-        nc.scalar.copy(a[0], a_ps[0][:])
-        for t in (2, 1, 3):
-            nc.vector.tensor_copy(a[t], a_ps[t][:])
         for t in range(2):
-            nc.scalar.activation(board[t][:].indirect(l3[:]), a[t], ACT.Copy)
-        for t in range(2, PACK):
-            nc.vector.tensor_copy(board[t][:].indirect(l3[:]), a[t])
-        for t in range(2):
-            fetch(t, 0, J)
-            nc.vector.tensor_tensor(diff[:, t, :], got[:, t, :], a[t], ALU.subtract)
-        for s in range(2):
-            js = slice(H * s, H * (s + 1))
-            for t in (2, 3):
-                fetch(t, H * s, H)
-                nc.vector.tensor_tensor(diff[:, t, js], got[:, t, js], a_ps[t][:, js], ALU.subtract)
-        hid = [new("hid%d" % s, [P, H * PACK], BF16) for s in range(2)]
+            fetch(t, whole)
+            nc.gpsimd.tensor_tensor(diff[:, t, :], got[:, t, :], a[t], ALU.subtract)
+        for t, slots in ((2, whole), (3, halves[0]), (3, halves[1])):
+            fetch(t, slots)
+            nc.vector.tensor_tensor(diff[:, t, slots], got[:, t, slots], a_ps[t][:, slots], ALU.subtract)
+
+        hid = [new("hid%d" % s, [P, HALF * PACK], BF16) for s in range(2)]
         for s in range(2):
             nc.scalar.activation(
-                hid[s][:].rearrange("p (c i t) -> p c t i", i=4, t=PACK),
-                diff[:, :, H * s : H * (s + 1)].rearrange("p t (c i) -> p c t i", i=4),
+                hid[s][:].rearrange("p (c i t) -> p c t i", i=LINE, t=PACK),
+                diff[:, :, halves[s]].rearrange("p t (c i) -> p c t i", i=LINE),
                 ACT.Abs,
             )
-        floor = sb.tile([P, 2, J], F32, name="floor", tag="a01", align_bytes=64)
-        for h in range(2):
-            nc.scalar.activation(floor[:, h, :], tz_rows[h][:].indirect(l5[:]), ACT.Copy, scale=so_cols[:, h : h + 1])
 
-        out_rows = out
+        floor = sb.tile([P, 2, J], F32, name="floor", tag="a01", align_bytes=ALIGN)
+        for h in range(2):
+            nc.scalar.activation(floor[:, h, :], tz_rows[h][:].indirect(by_entry[:]), ACT.Copy, scale=so_cols[:, h : h + 1])
+
         p_ps = [ps.tile([P, J], F32, name="p_ps%d" % h) for h in range(2)]
         for s in range(2):
-            hid_codes = new("hid_codes%d" % s, [P, H], U32)
-            hid_sc = new("hid_sc%d" % s, [P, H], U8)
+            hid_codes = new("hid_codes%d" % s, [P, HALF], U32)
+            hid_sc = new("hid_sc%d" % s, [P, HALF], U8)
             nc.vector.quantize_mx(hid_codes[:].bitcast(E5M2), hid_sc[:], hid[s][:])
             for h in range(2):
                 cols = slice(P * h, P * (h + 1))
                 nc.tensor.matmul_mx(
-                    p_ps[h][:, H * s : H * (s + 1)], lhsT=wb_codes[:, cols].bitcast(E4M3), lhsT_scale=wb_plane[:, cols],
+                    p_ps[h][:, halves[s]], lhsT=wb_codes[:, cols].bitcast(E4M3), lhsT_scale=wb_plane[:, cols],
                     rhs=hid_codes[:].bitcast(E5M2), rhs_scale=hid_sc[:], start=True, stop=True,
                 )
         for h in range(2):

from contextlib import ExitStack

import concourse.mybir as mybir

F32 = mybir.dt.float32
BF16 = mybir.dt.bfloat16
I32 = mybir.dt.int32
U32 = mybir.dt.uint32
U16 = mybir.dt.uint16
U8 = mybir.dt.uint8
E4M3 = mybir.dt.float8_e4m3fn_x4
E5M2 = mybir.dt.float8_e5m2_x4
E2M1 = mybir.dt.float4_e2m1fn_x4
ALU = mybir.AluOpType
ACT = mybir.ActivationFunctionType

K, F, T, Z, J, R, C, N, E = 512, 512, 1024, 1024, 256, 512, 512, 256, 1024
P = 128
PACK = 4
QUADS = 4
QUAD = 32
PER_COLUMN = 16
LINE = 4
HALF = J // 2
ALIGN = 64
FLOPS = 2 * K * R * J + 2 * F * R * J + 2 * R * N * J


def words_of(packed):
    return packed[0].rearrange("p n t -> p (n t)").bitcast(I32)


def rows_by_quadrant(scales):
    return scales[0].bitcast(I32).rearrange("(q i) n -> i q n", i=PACK)


def tile_list_boardownweighed_bank_one_stepfloor_kernel(
    tc, xt_words, xt_scales, w_words, w_scales, xo_words, xo_scales, w0_words, w0_scales, sa,
    wb_words, wb_scales, tz, so, offs, offs2, offs3, offs4, offs5, out,
):
    nc = tc.nc
    halves = [slice(HALF * s, HALF * (s + 1)) for s in range(2)]
    whole = slice(0, J)

    with ExitStack() as ctx:
        sb = ctx.enter_context(tc.tile_pool(name="sb", bufs=1))
        ps = ctx.enter_context(tc.psum_pool(name="ps", bufs=1))

        def new(name, shape, dtype):
            return sb.tile(shape, dtype, name=name, align_bytes=ALIGN)

        def load_list(name, src):
            entries = new(name, [P, J // PER_COLUMN], U16)
            nc.sync.dma_start(entries[:], src)
            return entries

        def offsets(entries, slots):
            return entries[:, slots.start // PER_COLUMN : slots.stop // PER_COLUMN]

        def load_plane(plane, scales):
            rows = scales[0].bitcast(I32)
            for q in range(QUADS):
                nc.sync.dma_start(plane[QUAD * q : QUAD * q + PACK, :].bitcast(I32), rows[PACK * q : PACK * (q + 1), :])

        def spread(plane, stage):
            for q in range(QUADS):
                nc.vector.tensor_copy(plane[QUAD * q : QUAD * q + PACK, :].bitcast(I32), stage[:, q, :])

        xt_plane = new("xt_plane", [P, T], U8)
        xo_plane = new("xo_plane", [P, Z], U8)
        ww_plane = new("ww_plane", [P, 2 * R], U8)
        wb_plane = new("wb_plane", [P, N], U8)
        board = [new("board%d" % t, [P, C], F32) for t in range(PACK)]
        nc.gpsimd.memset(xo_plane[:].bitcast(I32), 0)
        nc.vector.memset(xt_plane[:].bitcast(I32), 0)
        nc.vector.memset(ww_plane[:].bitcast(I32), 0)
        for t in range(PACK):
            (nc.vector, nc.gpsimd)[t // 2].memset(board[t][:], 0.0)
        nc.gpsimd.memset(wb_plane[:].bitcast(I32), 0)

        xt_stage = new("xt_stage", [PACK, QUADS, T // 4], I32)
        ww_stage = new("ww_stage", [PACK, QUADS, 2 * R // 4], I32)
        xt_tab = new("xt_tab", [P, T], U16)
        xo_tab = new("xo_tab", [P, Z], U32)
        w_raw = new("w_raw", [P, R], U32)
        w0_raw = new("w0_raw", [P, R], U32)
        tz_rows = [new("tz%d" % h, [P, E], F32) for h in range(2)]
        wb_codes = new("wb_codes", [P, N], U32)
        so_cols = new("so_cols", [P, 2], F32)
        sa_cols = new("sa_cols", [P, PACK], F32)

        by_token = load_list("by_token", offs)
        nc.sync.dma_start(ww_stage[:, :, 0 : R // 4], rows_by_quadrant(w_scales))
        nc.sync.dma_start(ww_stage[:, :, R // 4 : R // 2], rows_by_quadrant(w0_scales))
        nc.sync.dma_start(xt_stage[:], rows_by_quadrant(xt_scales))
        nc.sync.dma_start(xt_tab[:].bitcast(I32), xt_words[0].bitcast(I32))
        nc.sync.dma_start(w_raw[:].bitcast(I32), words_of(w_words))
        nc.sync.dma_start(xo_tab[:].bitcast(I32), words_of(xo_words))
        nc.sync.dma_start(w0_raw[:].bitcast(I32), words_of(w0_words))
        by_note = load_list("by_note", offs2)
        load_plane(xo_plane, xo_scales)
        to_board = load_list("to_board", offs3)
        from_board = load_list("from_board", offs4)
        nc.sync.dma_start(sa_cols[:], sa.rearrange("(p t) o -> p (t o)", t=PACK))
        for h in range(2):
            nc.sync.dma_start(tz_rows[h][:], tz[P * h : P * (h + 1), :])
        by_entry = load_list("by_entry", offs5)
        with nc.allow_non_contiguous_dma(reason="one value for each partition and half of the output rows"):
            nc.sync.dma_start(so_cols[:], so.rearrange("(h p) o -> p (h o)", p=P))
        nc.sync.dma_start(wb_codes[:].bitcast(I32), words_of(wb_words))
        load_plane(wb_plane, wb_scales)

        xt_codes = new("xt_codes", [P, J], U16)
        xt_sc = new("xt_sc", [P, J], U8)
        xo_codes = new("xo_codes", [P, J], U32)
        xo_sc = new("xo_sc", [P, J], U8)
        ww_sc = new("ww_sc", [P, 2, R], U8)
        spread(ww_plane, ww_stage)
        spread(xt_plane, xt_stage)
        nc.vector.tensor_copy(
            ww_sc[:].rearrange("p i (t m) -> p i t m", t=PACK),
            ww_plane[:].rearrange("p (i m t) -> p i t m", i=2, t=PACK),
        )
        nc.vector.tensor_copy(xt_sc[:], xt_plane[:].indirect(by_token[:]))
        nc.vector.tensor_copy(xt_codes[:], xt_tab[:].indirect(by_token[:]))
        for slots in halves:
            nc.vector.tensor_copy(xo_codes[:, slots], xo_tab[:].indirect(offsets(by_note, slots)))
            nc.vector.tensor_copy(xo_sc[:, slots], xo_plane[:].indirect(offsets(by_note, slots)))

        w_codes = new("w_codes", [P, R], U32)
        w0_codes = new("w0_codes", [P, R], U32)
        nc.scalar.copy(w_codes[:].rearrange("p (t m) -> p m t", t=PACK), w_raw[:].rearrange("p (m t) -> p m t", t=PACK))
        for u in range(2):
            nc.scalar.copy(
                w0_codes[:, 2 * P * u : 2 * P * (u + 1)].rearrange("p (t m) -> p m t", t=2),
                w0_raw[:].rearrange("p (m t) -> p m t", t=PACK)[:, :, 2 * u : 2 * u + 2],
            )

        products = ((w_codes, E5M2, xt_codes, E2M1, xt_sc), (w0_codes, E4M3, xo_codes, E5M2, xo_sc))

        def multiply(acc, t, i, slots):
            codes, fmt, picked, picked_fmt, picked_sc = products[i]
            nc.tensor.matmul_mx(
                acc[:], lhsT=codes[:, P * t : P * (t + 1)].bitcast(fmt), lhsT_scale=ww_sc[:, i, P * t : P * (t + 1)],
                rhs=picked[:, slots].bitcast(picked_fmt), rhs_scale=picked_sc[:, slots], start=(i == 0), stop=(i == 1),
            )

        a01 = new("a01", [P, 2, J], F32)
        a = [a01[:, 0, :], a01[:, 1, :]] + [new("a%d" % t, [P, J], F32)[:] for t in (2, 3)]
        a0_ps = [ps.tile([P, HALF], F32, name="a0_ps%d" % s) for s in range(2)]
        a_ps = {t: ps.tile([P, J], F32, name="a_ps%d" % t) for t in (1, 2)}
        for i in range(2):
            for s in range(2):
                multiply(a0_ps[s], 0, i, halves[s])
            for t in (1, 2):
                multiply(a_ps[t], t, i, whole)
        nc.scalar.copy(a01[:, 0, halves[0]], a0_ps[0][:])
        a_ps[3] = ps.tile([P, J], F32, name="a_ps3", tag="a0_ps0")
        for i in range(2):
            multiply(a_ps[3], 3, i, whole)
        nc.vector.tensor_copy(a01[:, 0, halves[1]], a0_ps[1][:])
        for t in range(1, PACK):
            nc.vector.tensor_copy(a[t], a_ps[t][:])

        for slots in halves:
            nc.scalar.activation(board[0][:].indirect(offsets(to_board, slots)), a01[:, 0, slots], ACT.Copy)
        nc.scalar.activation(board[2][:].indirect(to_board[:]), a[2], ACT.Copy)
        for t in (1, 3):
            nc.vector.tensor_copy(board[t][:].indirect(to_board[:]), a[t])

        got = new("got", [P, PACK, J], F32)
        diff = new("diff", [P, PACK, J], F32)

        def fetch(t, slots):
            nc.scalar.activation(
                got[:, t, slots], board[t][:].indirect(offsets(from_board, slots)), ACT.Copy, scale=sa_cols[:, t : t + 1]
            )

        for t in range(2):
            fetch(t, whole)
            nc.gpsimd.tensor_tensor(diff[:, t, :], got[:, t, :], a[t], ALU.subtract)
        for t, slots in ((2, whole), (3, halves[0]), (3, halves[1])):
            fetch(t, slots)
            nc.vector.tensor_tensor(diff[:, t, slots], got[:, t, slots], a_ps[t][:, slots], ALU.subtract)

        hid = [new("hid%d" % s, [P, HALF * PACK], BF16) for s in range(2)]
        for s in range(2):
            nc.scalar.activation(
                hid[s][:].rearrange("p (c i t) -> p c t i", i=LINE, t=PACK),
                diff[:, :, halves[s]].rearrange("p t (c i) -> p c t i", i=LINE),
                ACT.Abs,
            )

        floor = sb.tile([P, 2, J], F32, name="floor", tag="a01", align_bytes=ALIGN)
        for h in range(2):
            nc.scalar.activation(floor[:, h, :], tz_rows[h][:].indirect(by_entry[:]), ACT.Copy, scale=so_cols[:, h : h + 1])

        p_ps = [ps.tile([P, J], F32, name="p_ps%d" % h) for h in range(2)]
        for s in range(2):
            hid_codes = new("hid_codes%d" % s, [P, HALF], U32)
            hid_sc = new("hid_sc%d" % s, [P, HALF], U8)
            nc.vector.quantize_mx(hid_codes[:].bitcast(E5M2), hid_sc[:], hid[s][:])
            for h in range(2):
                cols = slice(P * h, P * (h + 1))
                nc.tensor.matmul_mx(
                    p_ps[h][:, halves[s]], lhsT=wb_codes[:, cols].bitcast(E4M3), lhsT_scale=wb_plane[:, cols],
                    rhs=hid_codes[:].bitcast(E5M2), rhs_scale=hid_sc[:], start=True, stop=True,
                )
        for h in range(2):
            y = new("y%d" % h, [P, J], F32)
            nc.vector.tensor_tensor(y[:], p_ps[h][:], floor[:, h, :], ALU.max)
            nc.sync.dma_start(out[P * h : P * (h + 1), :], y[:])
